import numpy as np, ml_dtypes
CORES = [3,7,11,15,131,135,139,143]
N = 8
BF = ml_dtypes.bfloat16
def f(rng, *shape):
    return (rng.standard_normal(shape, dtype=np.float32) * np.exp2(rng.integers(-2, 3, shape[:-1] + (1,)))).astype(BF)
def wide(rng, *shape):
    v = f(rng, *shape).astype(np.float32); k = shape[:-2] + (1, shape[-1])
    return (v * np.exp2(rng.integers(-6, 7, k)) * (rng.random(k) > 0.0625)).astype(BF)
def gentries(a):
    return np.ascontiguousarray(a.reshape(8, 16, -1).transpose(0, 2, 1)).reshape(8, -1)
def gtable(e):
    e = np.asarray(e); return np.ascontiguousarray(e.reshape(8, -1, 16).transpose(0, 2, 1)).reshape(128, -1).astype(np.int32)
T, M, K, L = 1536, 256, 12, 1
Z = T + N * M
def numbers_of(rng):
    return np.clip(2 * rng.standard_normal((N, 8, T)), -8, 8).astype(np.float32)
def pack(hf, ps, pd, S, E):
    return {"hf": hf, "ps": ps, "pd": pd, "sl": np.stack([gtable(S[q].reshape(8, N * M)) for q in range(N)]), "ed": np.stack([gtable(E[r].reshape(8, K * T)) for r in range(N)])}
def graph(rng):
    S = rng.integers(0, T, (N, 8, N, M)); sh = (N, 8, K, T)
    E = np.where(rng.random(sh) < 0.45, rng.integers(0, T, sh), rng.integers(T, Z, sh))
    share = rng.choice(np.array([0.0, 0.5, 0.9, 1.0]), (N, 8, 1, T), p=[0.02, 0.2, 0.3, 0.48])
    return S, np.where(rng.random(sh) < share, E, Z)
def setup_inputs(rng):
    S, E = graph(rng); return pack(f(rng, N, 128, T), numbers_of(rng), numbers_of(rng), S, E)
def setup_inputs_ends(rng):
    S, E = graph(rng); S = rng.choice(np.array([0, 1, T - 2, T - 1]), S.shape)
    c = rng.choice(np.array([0, T - 1, T, T + M - 1, T + M, Z - M, Z - 1, Z]), E.shape)
    return pack(f(rng, N, 128, T), numbers_of(rng), numbers_of(rng), S, np.where(rng.random(E.shape) < 0.9, c, E))
def setup_inputs_full(rng):
    S = np.argsort(rng.random((N, 8, N, T), dtype=np.float32), axis=-1)[..., :M]
    E = rng.integers(0, Z, (N, 8, K * T))
    for r in range(N):
        for g in range(8):
            E[r, g, rng.permutation(K * T)[:N * M]] = np.arange(T, Z)
    return pack(f(rng, N, 128, T), numbers_of(rng), numbers_of(rng), S, E.reshape(N, 8, K, T))
def setup_inputs_sparse(rng):
    S, E = graph(rng); E = np.where(rng.random(E.shape) * K < 0.8, E, Z); few = np.array([-8, -2, 0, 2, 8], np.float32)
    v = np.clip(f(rng, N, 128, T).astype(np.float32) * np.float32(2048), np.float32(-65536), np.float32(65536))
    v = np.where(rng.random((N, 1, T)) < 0.015625, np.copysign(np.float32(65536), v), v).astype(BF)
    return pack(v, rng.choice(few, (N, 8, T)), rng.choice(few, (N, 8, T)), S, E)
def setup_inputs_hub(rng):
    S, E = graph(rng); far = (np.arange(N).reshape(N, 1) + 1 + rng.integers(0, N - 1, (N, 8))) % N
    c = (T + far * M + rng.integers(0, M, (N, 8))).reshape(N, 8, 1, 1)
    E = np.where(rng.random(E.shape) < 0.5, c, E); E = np.where(rng.random((N, 8, 1, T)) < 0.125, c, E)
    return pack(f(rng, N, 128, T), numbers_of(rng), numbers_of(rng), S, E)
def setup_inputs_spread(rng):
    S, E = graph(rng); u = (rng.random((2, N, 8, T)) * 16 - 8).astype(np.float32)
    return pack(wide(rng, N, 128, T), u[0], u[1], S, E)
def check_inputs(d):
    bad = []
    if not (np.abs(d["hf"].astype(np.float32)) <= 65536).all(): bad.append("hf")
    for a in ("ps", "pd"):
        if not (np.abs(d[a]) <= 8).all(): bad.append(a)
    if not ((d["sl"] >= 0) & (d["sl"] < T)).all(): bad.append("sl")
    if not ((d["ed"] >= 0) & (d["ed"] <= Z)).all(): bad.append("ed")
    return bad
def reference(hf, ps, pd, sl, ed):
    S = np.stack([gentries(sl[q]) for q in range(N)]).reshape(N, 8, N, M); E = np.stack([gentries(ed[r]) for r in range(N)]).reshape(N, 8, K, T)
    x = hf.astype(np.float64).reshape(N, 8, 16, T); src = ps.astype(np.float64); dst = pd.astype(np.float64); wt = np.zeros((N, 8, K, T))
    for r in range(N):
        for g in range(8):
            t = np.concatenate([src[r, g]] + [src[q, g][S[q, g, r]] for q in range(N)] + [np.zeros(1)])
            z = t[E[r, g]] + dst[r, g]; w = np.where(E[r, g] < Z, np.exp(np.where(z >= 0, z, 0.25 * z)), 0.0)
            den = np.add.reduce(w, axis=0); wt[r, g] = w * np.reciprocal(np.where(den > 0, den, 1.0))
    for i in range(L):
        y = np.zeros((N, 8, 16, T))
        for r in range(N):
            for g in range(8):
                t = np.concatenate([x[r, g]] + [x[q, g][:, S[q, g, r]] for q in range(N)] + [np.zeros((16, 1))], axis=1)
                for k in range(K):
                    y[r, g] += wt[r, g, k] * t[:, E[r, g, k]]
        x = y
    return {"y": x.reshape(N, 128, T).astype(np.float32)}

@@ -1,0 +1,345 @@
+from concourse.bass import DstId, RemoteDMATransfer
+from concourse.mybir import AluOpType, AxisListType, ActivationFunctionType
+
+N, TN, M, K = 8, 1536, 256, 12
+Z = TN + N * M
+KS = K + 1
+QU = 32 * KS
+HU = 64 * KS
+GK = 8 * KS
+RING = 4
+CHUNKS = [(2, 0, 2), (2, 2, 2), (4, 0, 4), (4, 0, 4)]
+XR = [(0, 384), (384, 768), (768, 1024), (1024, 1280), (1280, 1536)]
+SK = [(0, 4), (4, 8), (8, 12)]
+
+SCRATCH = {
+    "xtab": ("sbuf", [128, 3600], "bfloat16"),
+    "stab": ("sbuf", [128, 3600], "bfloat16"),
+    "xs": ("sbuf", [128, N * M], "bfloat16"),
+    "ss": ("sbuf", [128, N * M], "bfloat16"),
+    "sl32": ("sbuf", [128, 128], "int32"),
+    "slo": ("sbuf", [128, 128], "uint16"),
+    "ed32": ("sbuf", [128, K, 96], "int32"),
+    "offx": ("sbuf", [128, K * 96], "uint16"),
+    "offs": ("sbuf", [128, K * 96], "uint16"),
+    "ps2": ("sbuf", [128, 96], "float32"),
+    "sp": ("sbuf", [128, TN], "bfloat16"),
+    "slp": ("sbuf", [128, 128], "uint16"),
+    "slf": ("sbuf", [128, 128], "float32"),
+    "sld": ("sbuf", [128, 128], "int32"),
+    "pa": ("sbuf", [128, 192], "int32"),
+    "pb": ("sbuf", [128, 96], "int32"),
+    "po": ("sbuf", [128, 96], "uint16"),
+    "pd8": ("sbuf", [8, TN], "float32"),
+    "ci": ("sbuf", [128, 672], "int32"),
+    "cj": ("sbuf", [128, 672], "int32"),
+    "cb": ("sbuf", [128, 672], "bfloat16"),
+    "id32": ("sbuf", [128, 8], "float32"),
+    "ones": ("sbuf", [128, GK], "float32"),
+    "big": ("sbuf", [128, 4], "float32"),
+    "zt": ("sbuf", [128, 24], "float32"),
+    "zc": ("sbuf", [128, 4], "float32"),
+    "pp": ("sbuf", [128, TN], "bfloat16"),
+    "f2": ("sbuf", [128, 12, 2, 8], "float32"),
+    "frep": ("sbuf", [128, 24 * GK], "float32"),
+    "xg": ("sbuf", [128, TN * KS], "bfloat16"),
+    "sg": ("sbuf", [128, TN * K], "bfloat16"),
+    "st": ("sbuf", [128, RING * 2 * HU], "float32"),
+    "tt": ("sbuf", [128, 4, 2 * GK], "float32"),
+    "wi": ("sbuf", [128, 4 * GK], "float32"),
+    "dn": ("sbuf", [128, 4 * GK], "float32"),
+    "rb": ("sbuf", [128, 12, 4, GK], "bfloat16"),
+    "rr": ("sbuf", [128, 12 * QU], "bfloat16"),
+    "yb": ("sbuf", [128, TN], "float32"),
+    "q": ("psum", [128, 4, 512], "float32"),
+    "b0": ("psum", [128, 1024], "float32"),
+    "b1": ("psum", [128, 1024], "float32"),
+}
+SEMAPHORES = ["cv", "cs", "ct", "cg", "l_sl", "l_hf", "l_ed", "l_p0", "l_p1", "l_pd", "xa", "sa", "sent", "stored"]
+
+ORDER = {
+    "v": "m_ones m_xz m_pp c_and c_eq o_c z_ai z_a o_d c_id o_e z_ci sl_1 slo sl_2 e_ic e_ia sl_3 p_hi z_sum p_r p_mid sl_4 "
+         "p_lo sl_5 p_t m_q sg3 f_i z_col offs3 offs2 offs1 b_and offs5 offs4 offx b_eq offs0 o_g1 x0_4 x0_7 x0_3 x0_0 x384_1 "
+         "x384_0 x0_8 x0_2 x384_7 s0_4 s1_4 s1_0 tt0 wi0 w0 r0 tt1 dn0 wi1 rc0 w1 hi0 r1 rm0 dn1 md0 rc1 lo0 tp0 rm1 s3_8 lo1 "
+         "sc0 sc1 tp1 sc2 tt2 sc3 w2 wi2 sc4 r2 sc5 dn2 rc2 sc7 rm2 md2 lo2 tp2 sc6 s5_4 sc8 sc9 sc10 sc11 tt3 wi3 w3 r3 dn3 "
+         "sc12 rc3 sc13 rm3 sc14 lo3 tp3 sc15 sc16 sc17 sc18 sc19 sc20 sc21 sc22 sc23 ex11",
+    "s": "ld_sl ld_p1 ld_pd z_big e_c1 e_a0 e_a1 e_c0 xg1 xg0 xg2 xg3 f_e xown sg1 sg0 sg2 o_g0 sown x768_9 x0_1 x0_11 "
+         "x768_11 x0_6 x0_5 x384_4 x384_6 s0_0 s0_8 s1_8 s2_4 s2_0 s3_0 s2_8 hi1 x0_10 x0_9 md1 x384_2 x384_9 x384_10 s3_4 "
+         "x384_8 s5_0 x384_11 x384_3 x384_5 x768_3 x1280_11 s4_8 hi2 x1280_6 x768_7 x768_5 s4_4 x768_0 s5_8 x768_4 s4_0 "
+         "x768_2 x768_10 x1024_1 x768_8 x768_6 x1024_4 x768_1 x1024_6 x1024_11 x1024_3 x1024_10 x1024_0 hi3 x1024_8 x1280_5 "
+         "md3 x1280_1 x1024_9 x1024_5 x1024_2 x1024_7 x1280_10 x1280_0 x1280_8 x1280_2 x1280_4 x1280_7 x1280_3 x1280_9 "
+         "ex7 ex8 ex9",
+    "t": "t_d cm0_4 cm0_0 cm0_8 cm1_4 cm1_8 cm1_0 cm2_0 bc0 bc1 cm2_4 cm2_8 bc2 cm3_8 cm3_0 cm3_4 bc3 bc4 bc5 bc7 bc6 cm4_8 "
+         "cm5_0 cm4_4 bc9 bc8 cm5_8 cm5_4 bc10 bc11 cm4_0 bc12 bc13 bc14 bc15 bc16 bc17 bc18 bc19 bc20 bc21 bc22 bc23",
+    "g": "i_id i_s o_a o_b i_b xsend0 xsend1 ssend0 ssend1 m_fr f_r0 f_r1 f_r2 f_r3 f_r4 f_r5 f_r6 f_r7 f_r8 f_r9 f_r10 "
+         "f_r11 m_rb m_xg ex0 ex2 ex1 ex3 ex5 ex6 ex4 ex10",
+    "y": "ld_p0 ld_hf ld_ed out1 out3 out5 out7 out9 out10 out11",
+}
+
+
+def exchange(src, cores, topo):
+    others = [d for d in range(len(cores)) if cores[d] != src]
+    far = [d for d in others if topo.host(cores[d]) != topo.host(src)]
+    home = [d for d in others if cores[d] in topo.cores_of(src)]
+    near = [d for d in others if d not in far and d not in home]
+    calls = []
+    used = set()
+    for grp in (far, near):
+        eng = topo.engines(src, cores[grp[0]])
+        n = len(eng) // len(grp)
+        calls.append([(d, sum(1 << e for e in eng[i * n:(i + 1) * n])) for i, d in enumerate(grp)])
+        used.update(eng)
+    free = [e for e in topo.engines(src, cores[home[0]]) if e not in used]
+    calls[1].append((home[0], sum(1 << e for e in free[::2])))
+    return calls, far, near, home
+
+
+def steps(g, core, T, topo):
+    rank = T.rank_of(core)
+    cores = list(T.cores)
+    S = T.sem
+    ACT, OP = ActivationFunctionType, AluOpType
+    V, A, PE = g.vector, g.scalar, g.tensor
+    tasks = {}
+
+    def add(name, deps, fn, n=1, tok=None):
+        tasks[name] = (list(deps), fn, n, tok)
+
+    def one(name, deps, fn):
+        add(name, deps, lambda e: [fn()])
+
+    def copy(name, deps, out, src, n=0):
+        def fn(e):
+            if e == "v":
+                return [V.tensor_copy(out, src)]
+            if e == "s":
+                return [A.activation(out, src, ACT.Copy)]
+            return [g.affine_select(out, src, [[0, n]], OP.is_ge, 0.0, 0, 0)]
+        add(name, deps, fn)
+
+    def zero(name, out, n):
+        add(name, [], lambda e: [V.memset(out, 0.0) if e == "v" else
+                                 g.iota(out, [[0, n]], 0, 0, allow_small_or_imprecise_dtypes=True)])
+
+    def dma(name, deps, out, src, sem, tok=True):
+        def fn(e):
+            (g.sync if e == "y" else A).dma_start(out, src).then_inc(sem, 16)
+            return []
+        add(name, deps, fn, 0, (sem, 16) if tok else None)
+
+    dma("ld_p0", [], T.ps2[:, 0:48], T.ps[0::2, :], S.l_p0)
+    dma("ld_p1", [], T.ps2[:, 48:96], T.ps[1::2, :], S.l_p1)
+    dma("ld_sl", [], T.sl32[:], T.sl[:], S.l_sl)
+    dma("ld_hf", [], T.xtab[:, 0:TN], T.hf[:], S.l_hf)
+    dma("ld_pd", [], T.pd8[:], T.pd[:], S.l_pd)
+    dma("ld_ed", ["ld_hf"], T.ed32[:], T.ed[:], S.l_ed)
+
+    sel = T.cb[:, 0:32]
+    one("i_id", [], lambda: g.iota(T.ci[:, 32:40], [[-32, 8]], 0, 32))
+    one("i_s", [], lambda: g.iota(T.ci[:, 0:32], [[-32, 4], [-128, 8]], 0, 8))
+    one("c_and", ["i_id", "i_s"], lambda: V.tensor_scalar(T.cj[:, 0:40], T.ci[:, 0:40], 0xFFE7, None, OP.bitwise_and))
+    one("c_id", ["c_and"], lambda: V.tensor_scalar(T.id32[:], T.cj[:, 32:40], 0.0, None, OP.is_equal))
+    one("c_eq", ["c_and"], lambda: V.tensor_scalar(sel, T.cj[:, 0:32], 0.0, None, OP.is_equal))
+    one("m_ones", [], lambda: V.memset(T.ones[:], 1.0))
+    zero("m_xz", T.xtab[:, Z:Z + 8], 8)
+    zero("m_pp", T.pp[:, 3::4], 384)
+    zero("m_xg", T.xg[:, K::KS], TN)
+    zero("m_rb", T.rb[:, :, 3, :], 12 * GK)
+    zero("m_fr", T.frep[:, K::KS], 192)
+    one("z_big", ["m_ones"], lambda: A.activation(T.big[:], T.ones[:, 0:4], ACT.Exp, scale=35.0))
+    one("z_a", ["c_eq"], lambda: V.tensor_scalar(T.zt[:, 0:8], T.cb[:, 0:8], 2.0 ** -42, None, OP.mult))
+    one("z_ai", ["c_eq"], lambda: V.tensor_scalar(T.zt[:, 8:16], T.cb[:, 24:32], 2.0 ** 38, None, OP.mult))
+    one("z_ci", ["c_eq", "z_big"], lambda: V.tensor_scalar(T.zt[:, 16:24], T.cb[:, 16:24], T.big[:, 0:1], None, OP.mult))
+    one("z_sum", ["z_a", "z_ai", "z_ci"], lambda: V.tensor_reduce(T.zc[:, 0:1], T.zt[:], AxisListType.X, OP.add))
+    one("z_col", ["z_sum", "m_ones"], lambda: V.tensor_scalar(T.stab[:, Z:Z + 8], T.ones[:, 0:8], T.zc[:, 0:1], None, OP.mult))
+
+    calls, far, near, home = exchange(core, cores, topo)
+    landed = 0
+    for c in cores:
+        if c != core:
+            for cl in exchange(c, cores, topo)[0]:
+                landed += sum(bin(m).count("1") for d, m in cl if d == rank)
+    one("slo", ["ld_sl"], lambda: V.tensor_copy(T.slo[:], T.sl32[:]))
+
+    def swap(tag, tab, own, off, stage, sem, deps):
+        made = {}
+        for grp in (far, near, home):
+            for i in range(0, len(grp), 2):
+                d, n = grp[i], len(grp[i:i + 2])
+                assert grp[i + n - 1] == d + n - 1
+                name = "%sg%d" % (tag, len(set(made.values())))
+                copy(name, deps, stage[:, d * M:(d + n) * M], own.indirect(off[:, d * 16:(d + n) * 16]))
+                for j in range(n):
+                    made[d + j] = name
+        block = tab[:, TN + rank * M:TN + (rank + 1) * M]
+        copy(tag + "own", deps, block, own.indirect(off[:, rank * 16:(rank + 1) * 16]))
+        for j, cl in enumerate(calls):
+            def fn(e, cl=cl):
+                trs = []
+                for d, m in cl:
+                    rid, pid = topo.addr(cores[d], core)
+                    trs.append(RemoteDMATransfer(dst_ids=[DstId(rid=rid, pnc=pid)], dma_engine_mask=m, remote_sem=sem,
+                                                 src=stage[:, d * M:(d + 1) * M], dst=block))
+                g.remote_dma_fused(trs, local_sem=S.sent)
+                return []
+            add("%ssend%d" % (tag, j), sorted(set(made[d] for d, m in cl)), fn, 0)
+        add(tag + "in", [], None, 0, (sem, landed))
+
+    swap("x", T.xtab, T.xtab[:, 0:TN], T.slo, T.xs, S.xa, ["ld_hf", "slo"])
+
+    ee, er = T.b0, T.b1
+    for x in range(2):
+        one("e_a%d" % x, ["ld_p%d" % x], lambda x=x: A.activation(ee[:, 4 * x:384:8], T.ps2[:, 48 * x:48 * x + 48], ACT.Exp))
+        one("e_c%d" % x, ["ld_p%d" % x],
+            lambda x=x: A.activation(ee[:, 4 * x + 1:384:8], T.ps2[:, 48 * x:48 * x + 48], ACT.Exp, scale=0.25))
+    exps = ["e_a0", "e_a1", "e_c0", "e_c1"]
+    one("e_ia", exps, lambda: V.reciprocal(ee[:, 3:384:4], ee[:, 0:384:4]))
+    one("e_ic", exps, lambda: V.reciprocal(ee[:, 2:384:4], ee[:, 1:384:4]))
+    one("p_hi", ["e_ia", "e_ic"], lambda: V.tensor_copy(T.pp[:, 0::4], ee[:, 0:384]))
+    one("p_r", ["p_hi"], lambda: V.tensor_tensor(er[:, 0:384], ee[:, 0:384], T.pp[:, 0::4], OP.subtract))
+    one("p_mid", ["p_r"], lambda: V.tensor_copy(T.pp[:, 1::4], er[:, 0:384]))
+    one("p_lo", ["p_mid"], lambda: V.tensor_tensor(T.pp[:, 2::4], er[:, 0:384], T.pp[:, 1::4], OP.subtract))
+    one("p_t", ["p_lo", "m_pp"], lambda: V.transpose(T.sp[:], T.pp[:]))
+    one("sl_1", ["ld_sl"], lambda: V.tensor_scalar(T.slf[:], T.sl32[:], 1.0 / 48, -23.5 / 48, OP.mult, OP.add))
+    one("sl_2", ["sl_1"], lambda: V.tensor_copy(T.sld[:], T.slf[:]))
+    one("sl_3", ["sl_2"], lambda: V.tensor_scalar(T.slf[:], T.sld[:], -47.96875, None, OP.mult))
+    one("sl_4", ["sl_3"], lambda: V.tensor_tensor(T.slf[:], T.slf[:], T.sl32[:], OP.add))
+    one("sl_5", ["sl_4"], lambda: V.tensor_scalar(T.slp[:], T.slf[:], 32.0, None, OP.mult))
+    swap("s", T.stab, T.sp[:, 0:TN], T.slp, T.ss, S.sa, ["p_t", "sl_5"])
+    one("o_a", [], lambda: g.iota(T.pa[:, 0:96], [[1, 32], [0, 3]], 0, 32))
+    one("o_b", [], lambda: g.iota(T.pa[:, 96:192], [[0, 32], [512, 3]], 0, 0))
+    one("o_c", ["o_a"], lambda: V.tensor_scalar(T.pb[:], T.pa[:, 0:96], 511, None, OP.bitwise_and))
+    one("o_d", ["o_b", "o_c"], lambda: V.tensor_tensor(T.pb[:], T.pb[:], T.pa[:, 96:192], OP.add))
+    one("o_e", ["o_d"], lambda: V.tensor_copy(T.po[:], T.pb[:]))
+    for i in range(2):
+        copy("o_g%d" % i, ["p_t", "o_e"], T.stab[:, i * 768:(i + 1) * 768], T.sp[:, 0:TN].indirect(T.po[:, i * 48:(i + 1) * 48]))
+
+    add("t_d", ["ld_pd", "c_id"],
+        lambda e: [PE.transpose(T.q[:, 0, 416 + t * 8:424 + t * 8], T.pd8[:, t * 128:(t + 1) * 128], T.id32[0:8, 0:8])
+                   for t in range(12)], 12)
+    one("f_e", ["t_d"], lambda: A.activation(T.f2[:, :, 0, :], T.q[:, 0, 416:512], ACT.Exp, scale=-0.75))
+    one("m_q", ["f_e"], lambda: V.memset(T.q[:, :, K:4 * GK:KS], 0.0))
+    one("f_i", ["f_e"], lambda: V.reciprocal(T.f2[:, :, 1, :], T.f2[:, :, 0, :]))
+    for k in range(K):
+        copy("f_r%d" % k, ["f_i"], T.frep[:, k::KS], T.f2[:], 192)
+    frep = ["f_r%d" % k for k in range(K)] + ["m_fr"]
+    one("offx", ["ld_ed"], lambda: V.tensor_copy(T.offx[:], T.ed32[:]))
+    for p in range(6):
+        one("offs%d" % p, ["ld_ed"],
+            lambda p=p: V.tensor_copy(T.offs[:, p * 192:(p + 1) * 192], T.ed32[:, :, p * 16:(p + 1) * 16]))
+    one("i_b", [], lambda: g.iota(T.ci[:, 160:672], [[-32, 4], [-1, 8], [0, 16]], 0, 1))
+    one("b_and", ["i_b"], lambda: V.tensor_scalar(T.cj[:, 160:672], T.ci[:, 160:672], 0xFFE7, None, OP.bitwise_and))
+    one("b_eq", ["b_and"], lambda: V.tensor_scalar(T.cb[:, 160:672], T.cj[:, 160:672], 0.0, None, OP.is_equal))
+
+    for a, b in XR:
+        for k in range(K):
+            copy("x%d_%d" % (a, k), ["xin", "xown", "m_xz", "offx"], T.xg[:, a * KS + k:b * KS:KS],
+                 T.xtab[:, 0:Z + 8].indirect(T.offx[:, k * 96 + a // 16:k * 96 + b // 16]))
+    for p in range(6):
+        for a, b in SK:
+            copy("s%d_%d" % (p, a), ["sin", "sown", "o_g0", "o_g1", "z_col", "offs%d" % p],
+                 T.sg[:, (p * K + a) * 256:(p * K + b) * 256],
+                 T.stab[:, 0:Z + 8].indirect(T.offs[:, (p * K + a) * 16:(p * K + b) * 16]))
+
+    last = ["m_q"] * 4
+
+    def ratios(s, t0, nt, o):
+        qa, qw, qr, qi = [T.q[:, o:o + nt, i * GK:(i + 1) * GK] for i in range(4)]
+        wi = T.wi[:, o * GK:(o + nt) * GK]
+        hi, mid, lo = [T.rb[:, t0:t0 + nt, j, :] for j in range(3)]
+        cms = []
+        for p in range(t0 // 2, (t0 + nt) // 2):
+            bank = o + 2 * p - t0
+            for a, b in SK:
+                cms.append("cm%d_%d" % (p, a))
+                add(cms[-1], ["s%d_%d" % (p, a), "c_eq", last[bank]],
+                    lambda e, a=a, b=b, p=p, bank=bank: [
+                        PE.matmul(T.q[:, bank + j, k:4 * GK:KS],
+                                  T.sg[:, (p * K + k) * 256 + j * 128:(p * K + k) * 256 + (j + 1) * 128], sel, True, True)
+                        for k in range(a, b) for j in range(2)], 2 * (b - a))
+            last[bank] = "lo" + s
+        one("tt" + s, cms + frep, lambda: V.tensor_tensor(T.tt[:, o:o + nt, :], T.q[:, o:o + nt, GK:3 * GK],
+                                                          T.frep[:, t0 * 2 * GK:(t0 + nt) * 2 * GK], OP.mult))
+        one("w" + s, ["tt" + s], lambda: V.tensor_tensor(qw, qa, T.tt[:, o:o + nt, 0:GK], OP.max))
+        one("wi" + s, ["tt" + s], lambda: V.tensor_tensor(wi, qi, T.tt[:, o:o + nt, GK:2 * GK], OP.min))
+        one("r" + s, ["w" + s, "wi" + s], lambda: V.tensor_tensor(qr, T.q[:, o:o + nt, GK - 1:2 * GK - 1], wi, OP.mult))
+        add("dn" + s, ["r" + s, "m_ones"],
+            lambda e: [V.tensor_tensor_scan(T.dn[:, j * GK:(j + 1) * GK], T.q[:, j, 2 * GK:3 * GK], T.ones[:],
+                                            0.0, OP.mult, OP.add) for j in range(o, o + nt)], nt)
+        one("rc" + s, ["dn" + s],
+            lambda: V.reciprocal(T.q[:, o:o + nt, 2 * GK + K:3 * GK:KS], T.dn[:, o * GK + K - 1:(o + nt) * GK:KS]))
+        copy("hi" + s, ["rc" + s], hi, qr)
+        one("rm" + s, ["hi" + s], lambda: V.tensor_tensor(qw, qr, hi, OP.subtract))
+        copy("md" + s, ["rm" + s], mid, qw)
+        one("lo" + s, ["md" + s], lambda: V.tensor_tensor(lo, qw, mid, OP.subtract))
+
+    t0 = 0
+    for c, (nt, o, turn) in enumerate(CHUNKS):
+        ratios("%d" % c, t0, nt, o)
+        t0 += nt
+        if not turn:
+            continue
+        t1 = t0 - turn
+        add("tp%d" % c, ["lo%d" % c, "m_rb"] + (["lo%d" % (c - 1)] if turn > nt else []),
+            lambda e, t0=t0, t1=t1: [V.transpose(T.rr[:, t1 * QU + k:t0 * QU:KS], T.rb[:, t1:t0, :, k::KS]) for k in range(KS)], KS)
+        for t in range(t1, t0):
+            w = 2 * (t % RING) * HU
+            for h in range(2):
+                u = 2 * t + h
+                buf = T.b1 if h else T.b0
+                add("bc%d" % u, ["tp%d" % c, "b_eq"] + (["sc%d" % (u - 2)] if u >= 2 else []),
+                    lambda e, buf=buf, o=t * QU, h=h: [
+                        PE.matmul(buf[:, j * QU + a:j * QU + b], T.cb[:, 160 + (2 * h + j) * 128:288 + (2 * h + j) * 128],
+                                  T.rr[:, o + a:o + b], True, True)
+                        for j, a, b in ((0, 0, QU), (1, 0, 512 - QU), (1, 512 - QU, QU))], 3)
+                a = [a for a, b in XR if a <= u * 64 < b][0]
+                one("sc%d" % u, ["bc%d" % u, "m_xg"] + ["x%d_%d" % (a, k) for k in range(K)]
+                    + (["ex%d" % (t - RING)] if t >= RING else []),
+                    lambda u=u, buf=buf, w=w + h * HU: V.tensor_tensor_scan(T.st[:, w:w + HU], buf[:, 0:HU],
+                                                                            T.xg[:, u * HU:(u + 1) * HU], 0.0, OP.mult, OP.add))
+            copy("ex%d" % t, ["sc%d" % (2 * t), "sc%d" % (2 * t + 1)], T.yb[:, t * 128:(t + 1) * 128],
+                 T.st[:, w + K:w + 2 * HU:KS], 128)
+            if t % 2 or t >= 10:
+                a, b = (t if t >= 10 else t - 1) * 128, (t + 1) * 128
+                dma("out%d" % t, ["ex%d" % i for i in range(a // 128, t + 1)], T.y[:, a:b], T.yb[:, a:b], S.stored, False)
+    sent = 2 * sum(bin(m).count("1") for cl in calls for d, m in cl)
+    return tasks, sent
+
+
+def rank_program(g, core, T, topo):
+    if T.rank_of(core) is None:
+        return
+    S = T.sem
+    tasks, sent = steps(g, core, T, topo)
+    queues = {e: ORDER[e].split() for e in ORDER}
+    cnt = {"v": S.cv, "s": S.cs, "t": S.ct, "g": S.cg}
+    token = {}
+    total = {}
+    for e in queues:
+        n = 0
+        for name in queues[e]:
+            if tasks[name][2]:
+                n += tasks[name][2]
+                token[name] = (e, cnt[e], n)
+        total[e] = n
+    for name in tasks:
+        if tasks[name][3] is not None:
+            token[name] = (name,) + tasks[name][3]
+    engine = {"v": g.vector, "s": g.scalar, "t": g.tensor, "g": g, "y": g.sync}
+    for e in queues:
+        seen = {}
+        for name in queues[e]:
+            need = {}
+            for d in tasks[name][0]:
+                k, sem, n = token[d]
+                if n > seen.get(k, 0) and n > need.get(k, (None, 0))[1]:
+                    need[k] = (sem, n)
+            for k in need:
+                engine[e].wait_ge(need[k][0], need[k][1])
+                seen[k] = need[k][1]
+            for ins in tasks[name][1](e):
+                ins.then_inc(cnt[e], 1)
+    for e in "vstg":
+        g.wait_ge(cnt[e], total[e])
+    g.wait_ge(S.sent, sent)
+    g.wait_ge(S.stored, 16 * len([n for n in tasks if n.startswith("out")]))

@@ -8,9 +8,29 @@ QU = 32 * KS
 HU = 64 * KS
 GK = 8 * KS
 RING = 4
-CHUNKS = [(2, 0, 2), (2, 2, 2), (4, 0, 4), (4, 0, 4)]
-XR = [(0, 384), (384, 768), (768, 1024), (1024, 1280), (1280, 1536)]
-SK = [(0, 4), (4, 8), (8, 12)]
+NT = 3
+NC = 12 // NT
+CN = 128 * NT
+CL = CN // 16
+TURNS = [(0, 1), (1, 3), (3, 4)]
+XR = [[(0, CN)], [(0, CN)], [(0, CN)], [(0, 256), (256, CN)]]
+SK = [(0, 3), (3, 6), (6, 9), (9, 12)]
+GATHERS = "s0 s1 x0 s2 s3 x1 x2 x3"
+GATHER, CALL, TENSOR, WAKE, PATIENCE, PARTS = 1.6, 70, 1.0, 170, 200, 5000
+LO, MD = "vvvv", "ssss"
+SHORT = 15
+SOON = 300
+FIRST = 8
+WIDE = 1
+SHARE = 0.23
+START = {
+    "v": "m_ones m_xz m_pp m_fr m_rb b_and c_and b_eq slo c_eq c_neg z_a z_ai z_ci xg1 iat ict z_sum iau icu z_col ia ic "
+         "p_hi0 p_hi1 p_r0 p_hi2 p_mid0 p_r1 p_lo0 p_mid1 p_r2 p_lo1 p_mid2 f_it p_lo2 f_iu f_i off0 p_c2 sg1 sg3 m_q off1 off2 off3",
+    "s": "ld_sl z_big c_id32 e_c e_yc e_a e_ya xg0 xg2 xg3 f_e f_y xown p_c0 p_c1 sg0 sg2 sown",
+    "t": "t_s t_d p_t0 p_t1 p_t2",
+    "g": "i_b c_perm i_s c_id xsend0 xsend1 ssend0 ssend1 f_r0 f_r1 f_r2 f_r3 f_r4 f_r5 f_r6 f_r7 f_r8 f_r9 f_r10 f_r11 m_xg",
+    "y": "ld_ps ld_hf ld_pd ld_ed out1 out3 out5 out7 out9 out10 out11",
+}
 
 SCRATCH = {
     "xtab": ("sbuf", [128, 3600], "bfloat16"),
@@ -20,22 +40,19 @@ SCRATCH = {
     "sl32": ("sbuf", [128, 128], "int32"),
     "slo": ("sbuf", [128, 128], "uint16"),
     "ed32": ("sbuf", [128, K, 96], "int32"),
-    "offx": ("sbuf", [128, K * 96], "uint16"),
-    "offs": ("sbuf", [128, K * 96], "uint16"),
-    "ps2": ("sbuf", [128, 96], "float32"),
-    "sp": ("sbuf", [128, TN], "bfloat16"),
-    "slp": ("sbuf", [128, 128], "uint16"),
-    "slf": ("sbuf", [128, 128], "float32"),
-    "sld": ("sbuf", [128, 128], "int32"),
-    "pa": ("sbuf", [128, 192], "int32"),
-    "pb": ("sbuf", [128, 96], "int32"),
-    "po": ("sbuf", [128, 96], "uint16"),
-    "pd8": ("sbuf", [8, TN], "float32"),
-    "ci": ("sbuf", [128, 672], "int32"),
-    "cj": ("sbuf", [128, 672], "int32"),
-    "cb": ("sbuf", [128, 672], "bfloat16"),
-    "id32": ("sbuf", [128, 8], "float32"),
-    "ones": ("sbuf", [128, GK], "float32"),
+    "off": ("sbuf", [128, K * 96], "uint16"),
+    "p96": ("sbuf", [128, 128], "float32"),
+    "d96": ("sbuf", [128, 128], "float32"),
+    "turn": ("sbuf", [128, 96], "float32"),
+    "ident": ("sbuf", [128, 128], "bfloat16"),
+    "neg": ("sbuf", [128, 128], "bfloat16"),
+    "id32": ("sbuf", [128, 128], "float32"),
+    "y0": ("sbuf", [128, 384], "float32"),
+    "r32": ("sbuf", [128, 12 * GK], "float32"),
+    "ci": ("sbuf", [128, 544], "int32"),
+    "cj": ("sbuf", [128, 544], "int32"),
+    "cb": ("sbuf", [128, 544], "bfloat16"),
+    "ones": ("sbuf", [128, NT * GK], "float32"),
     "big": ("sbuf", [128, 4], "float32"),
     "zt": ("sbuf", [128, 24], "float32"),
     "zc": ("sbuf", [128, 4], "float32"),
@@ -45,36 +62,82 @@ SCRATCH = {
     "xg": ("sbuf", [128, TN * KS], "bfloat16"),
     "sg": ("sbuf", [128, TN * K], "bfloat16"),
     "st": ("sbuf", [128, RING * 2 * HU], "float32"),
-    "tt": ("sbuf", [128, 4, 2 * GK], "float32"),
-    "wi": ("sbuf", [128, 4 * GK], "float32"),
-    "dn": ("sbuf", [128, 4 * GK], "float32"),
+    "tt": ("sbuf", [128, NT, 2 * GK], "float32"),
+    "wi": ("sbuf", [128, NT * GK], "float32"),
+    "dn": ("sbuf", [128, NT * GK], "float32"),
     "rb": ("sbuf", [128, 12, 4, GK], "bfloat16"),
     "rr": ("sbuf", [128, 12 * QU], "bfloat16"),
     "yb": ("sbuf", [128, TN], "float32"),
-    "q": ("psum", [128, 4, 512], "float32"),
+    "q": ("psum", [128, NT, 512], "float32"),
+    "rq": ("psum", [128, 512], "float32"),
     "b0": ("psum", [128, 1024], "float32"),
     "b1": ("psum", [128, 1024], "float32"),
 }
-SEMAPHORES = ["cv", "cs", "ct", "cg", "l_sl", "l_hf", "l_ed", "l_p0", "l_p1", "l_pd", "xa", "sa", "sent", "stored"]
+SEMAPHORES = ["cv", "cs", "ct", "cg", "l_sl", "l_hf", "l_ed", "l_ps", "l_pd", "xa", "sa", "sent", "stored"]
 
-ORDER = {
-    "v": "m_ones m_xz m_pp c_and c_eq o_c z_ai z_a o_d c_id o_e z_ci sl_1 slo sl_2 e_ic e_ia sl_3 p_hi z_sum p_r p_mid sl_4 "
-         "p_lo sl_5 p_t m_q sg3 f_i z_col offs3 offs2 offs1 b_and offs5 offs4 offx b_eq offs0 o_g1 x0_4 x0_7 x0_3 x0_0 x384_1 "
-         "x384_0 x0_8 x0_2 x384_7 s0_4 s1_4 s1_0 tt0 wi0 w0 r0 tt1 dn0 wi1 rc0 w1 hi0 r1 rm0 dn1 md0 rc1 lo0 tp0 rm1 s3_8 lo1 "
-         "sc0 sc1 tp1 sc2 tt2 sc3 w2 wi2 sc4 r2 sc5 dn2 rc2 sc7 rm2 md2 lo2 tp2 sc6 s5_4 sc8 sc9 sc10 sc11 tt3 wi3 w3 r3 dn3 "
-         "sc12 rc3 sc13 rm3 sc14 lo3 tp3 sc15 sc16 sc17 sc18 sc19 sc20 sc21 sc22 sc23 ex11",
-    "s": "ld_sl ld_p1 ld_pd z_big e_c1 e_a0 e_a1 e_c0 xg1 xg0 xg2 xg3 f_e xown sg1 sg0 sg2 o_g0 sown x768_9 x0_1 x0_11 "
-         "x768_11 x0_6 x0_5 x384_4 x384_6 s0_0 s0_8 s1_8 s2_4 s2_0 s3_0 s2_8 hi1 x0_10 x0_9 md1 x384_2 x384_9 x384_10 s3_4 "
-         "x384_8 s5_0 x384_11 x384_3 x384_5 x768_3 x1280_11 s4_8 hi2 x1280_6 x768_7 x768_5 s4_4 x768_0 s5_8 x768_4 s4_0 "
-         "x768_2 x768_10 x1024_1 x768_8 x768_6 x1024_4 x768_1 x1024_6 x1024_11 x1024_3 x1024_10 x1024_0 hi3 x1024_8 x1280_5 "
-         "md3 x1280_1 x1024_9 x1024_5 x1024_2 x1024_7 x1280_10 x1280_0 x1280_8 x1280_2 x1280_4 x1280_7 x1280_3 x1280_9 "
-         "ex7 ex8 ex9",
-    "t": "t_d cm0_4 cm0_0 cm0_8 cm1_4 cm1_8 cm1_0 cm2_0 bc0 bc1 cm2_4 cm2_8 bc2 cm3_8 cm3_0 cm3_4 bc3 bc4 bc5 bc7 bc6 cm4_8 "
-         "cm5_0 cm4_4 bc9 bc8 cm5_8 cm5_4 bc10 bc11 cm4_0 bc12 bc13 bc14 bc15 bc16 bc17 bc18 bc19 bc20 bc21 bc22 bc23",
-    "g": "i_id i_s o_a o_b i_b xsend0 xsend1 ssend0 ssend1 m_fr f_r0 f_r1 f_r2 f_r3 f_r4 f_r5 f_r6 f_r7 f_r8 f_r9 f_r10 "
-         "f_r11 m_rb m_xg ex0 ex2 ex1 ex3 ex5 ex6 ex4 ex10",
-    "y": "ld_p0 ld_hf ld_ed out1 out3 out5 out7 out9 out10 out11",
-}
+
+def order(tasks):
+    xs = [["x%d_%d_%d" % (c, a, k) for a, b in XR[c] for k in range(K)] for c in range(NC)]
+    ss = [["s%d_%d" % (c, a) for a, b in SK] for c in range(NC)]
+    lists = {"x": xs, "s": ss}
+    gathers = [n for part in GATHERS.split() for n in lists[part[0]][int(part[1])]]
+    cost = {}
+    for c in range(NC):
+        for a, b in XR[c]:
+            cost.update({"x%d_%d_%d" % (c, a, k): CALL + GATHER * (b - a) for k in range(K)})
+        for a, b in SK:
+            cost["s%d_%d" % (c, a)] = CALL + GATHER * CN * (b - a)
+            cost["cm%d_%d" % (c, a)] = TENSOR * 64 * NT * (b - a)
+        for n, w in (("tt", 2), ("w", 1), ("wi", 1), ("r", 1), ("dn", 1), ("rc", 1.2), ("md", 1.25), ("lo", 1), ("hi", 2.7),
+                     ("rm", 5 * TENSOR)):
+            cost[n + str(c)] = w * NT * GK + SHORT
+    for i, (a, b) in enumerate(TURNS):
+        cost["tp%d" % i] = KS * (max(64, 16 * NT * (b - a)) + SHORT)
+    scans = 48 // WIDE
+    for u in range(scans):
+        cost["sc%d" % u], cost["bc%d" % u], cost["ex%d" % (u % 12)] = WIDE * QU + SHORT, TENSOR * WIDE * QU, 510
+
+    def each(names, n):
+        return [a + str(i) for i in range(n) for a in names.split()]
+    own = each("lo", NC) + each("tp", len(TURNS)) + each("tt w wi r dn rc", NC) + each("sc", scans) + ["ex11"]
+    first = xs[0][:FIRST]
+    prefer = {"v": own + first + gathers, "s": each("md", NC) + [n for n in gathers if n not in first],
+              "t": each("rm", NC) + ["cm" + n[1:] for c in ss for n in c] + each("bc", scans), "g": each("hi", NC) + each("ex", 11)}
+    for c in range(NC):
+        if LO[c] == "s":
+            prefer["v"].remove("lo%d" % c)
+            prefer["s"].insert(0, "lo%d" % c)
+            prefer["t"].insert(0, "rl%d" % c)
+            cost["rl%d" % c] = TENSOR * NT * GK
+        if MD[c] == "v":
+            prefer["s"].remove("md%d" % c)
+            prefer["v"].insert(0, "md%d" % c)
+    queues = {e: START[e].split() for e in START}
+    done = {n: 0 for e in queues for n in queues[e]}
+    done["xin"], done["sin"] = 0, PARTS
+    free = {e: 0 for e in prefer}
+    left = set(cost)
+    share = SHARE * sum(cost[n] for n in gathers)
+    while left:
+        e = min(free, key=lambda k: free[k])
+        ready = {n: max(done[d] for d in tasks[n][0]) + WAKE for n in prefer[e]
+                 if n in left and all(d in done for d in tasks[n][0])}
+        now = [n for n in prefer[e] if n in ready and ready[n] <= free[e] + (PATIENCE if n not in gathers else 0)]
+        if e == "v" and share <= 0:
+            now = [n for n in now if n not in gathers]
+        if e == "v" and any(ready[n] <= free[e] + SOON for n in ready if n not in gathers):
+            now = [n for n in now if n not in lists["s"][0] + lists["s"][1] + lists["s"][2] + lists["s"][3]]
+        now = [n for n in now if ready[n] <= free[e] and n not in gathers] + now
+        if not now:
+            free[e] += 20
+            continue
+        n = now[0]
+        if e == "v" and n in gathers:
+            share -= cost[n]
+        free[e] = done[n] = max(free[e], ready[n]) + cost[n]
+        queues[e].append(n)
+        left.remove(n)
+    return queues
 
 
 def exchange(src, cores, topo):
@@ -117,7 +180,7 @@ def steps(g, core, T, topo):
             return [g.affine_select(out, src, [[0, n]], OP.is_ge, 0.0, 0, 0)]
         add(name, deps, fn)
 
-    def zero(name, out, n):
+    def zero(name, out, n=0):
         add(name, [], lambda e: [V.memset(out, 0.0) if e == "v" else
                                  g.iota(out, [[0, n]], 0, 0, allow_small_or_imprecise_dtypes=True)])
 
@@ -127,25 +190,26 @@ def steps(g, core, T, topo):
             return []
         add(name, deps, fn, 0, (sem, 16) if tok else None)
 
-    dma("ld_p0", [], T.ps2[:, 0:48], T.ps[0::2, :], S.l_p0)
-    dma("ld_p1", [], T.ps2[:, 48:96], T.ps[1::2, :], S.l_p1)
+    dma("ld_ps", [], T.p96[0:96, :], T.ps[:], S.l_ps)
+    dma("ld_pd", [], T.d96[0:96, :], T.pd[:], S.l_pd)
     dma("ld_sl", [], T.sl32[:], T.sl[:], S.l_sl)
     dma("ld_hf", [], T.xtab[:, 0:TN], T.hf[:], S.l_hf)
-    dma("ld_pd", [], T.pd8[:], T.pd[:], S.l_pd)
     dma("ld_ed", ["ld_hf"], T.ed32[:], T.ed[:], S.l_ed)
 
     sel = T.cb[:, 0:32]
-    one("i_id", [], lambda: g.iota(T.ci[:, 32:40], [[-32, 8]], 0, 32))
-    one("i_s", [], lambda: g.iota(T.ci[:, 0:32], [[-32, 4], [-128, 8]], 0, 8))
-    one("c_and", ["i_id", "i_s"], lambda: V.tensor_scalar(T.cj[:, 0:40], T.ci[:, 0:40], 0xFFE7, None, OP.bitwise_and))
-    one("c_id", ["c_and"], lambda: V.tensor_scalar(T.id32[:], T.cj[:, 32:40], 0.0, None, OP.is_equal))
-    one("c_eq", ["c_and"], lambda: V.tensor_scalar(sel, T.cj[:, 0:32], 0.0, None, OP.is_equal))
     one("m_ones", [], lambda: V.memset(T.ones[:], 1.0))
-    zero("m_xz", T.xtab[:, Z:Z + 8], 8)
-    zero("m_pp", T.pp[:, 3::4], 384)
+    one("c_perm", ["m_ones"], lambda: g.affine_select(T.turn[:], T.ones[:, 0:96], [[-1, 12], [-12, 8]], OP.is_equal, 0.0, 0, 1))
+    one("c_id", ["m_ones"], lambda: g.affine_select(T.ident[:], T.ones[:, 0:128], [[-1, 128]], OP.is_equal, 0.0, 0, 1))
+    one("c_neg", ["c_id"], lambda: V.tensor_scalar(T.neg[:], T.ident[:], -1.0, None, OP.mult))
+    copy("c_id32", ["c_id"], T.id32[:], T.ident[:])
+    one("i_s", [], lambda: g.iota(T.ci[:, 0:32], [[-32, 4], [-128, 8]], 0, 8))
+    one("c_and", ["i_s"], lambda: V.tensor_scalar(T.cj[:, 0:32], T.ci[:, 0:32], 0xFFE7, None, OP.bitwise_and))
+    one("c_eq", ["c_and"], lambda: V.tensor_scalar(sel, T.cj[:, 0:32], 0.0, None, OP.is_equal))
+    zero("m_xz", T.xtab[:, Z:Z + 8])
+    zero("m_pp", T.pp[:, 3::4])
     zero("m_xg", T.xg[:, K::KS], TN)
     zero("m_rb", T.rb[:, :, 3, :], 12 * GK)
-    zero("m_fr", T.frep[:, K::KS], 192)
+    zero("m_fr", T.frep[:, K::KS])
     one("z_big", ["m_ones"], lambda: A.activation(T.big[:], T.ones[:, 0:4], ACT.Exp, scale=35.0))
     one("z_a", ["c_eq"], lambda: V.tensor_scalar(T.zt[:, 0:8], T.cb[:, 0:8], 2.0 ** -42, None, OP.mult))
     one("z_ai", ["c_eq"], lambda: V.tensor_scalar(T.zt[:, 8:16], T.cb[:, 24:32], 2.0 ** 38, None, OP.mult))
@@ -161,18 +225,19 @@ def steps(g, core, T, topo):
                 landed += sum(bin(m).count("1") for d, m in cl if d == rank)
     one("slo", ["ld_sl"], lambda: V.tensor_copy(T.slo[:], T.sl32[:]))
 
-    def swap(tag, tab, own, off, stage, sem, deps):
+    def swap(tag, tab, stage, sem, deps):
+        own = tab[:, 0:TN]
         made = {}
         for grp in (far, near, home):
             for i in range(0, len(grp), 2):
                 d, n = grp[i], len(grp[i:i + 2])
                 assert grp[i + n - 1] == d + n - 1
                 name = "%sg%d" % (tag, len(set(made.values())))
-                copy(name, deps, stage[:, d * M:(d + n) * M], own.indirect(off[:, d * 16:(d + n) * 16]))
+                copy(name, deps, stage[:, d * M:(d + n) * M], own.indirect(T.slo[:, d * 16:(d + n) * 16]))
                 for j in range(n):
                     made[d + j] = name
         block = tab[:, TN + rank * M:TN + (rank + 1) * M]
-        copy(tag + "own", deps, block, own.indirect(off[:, rank * 16:(rank + 1) * 16]))
+        copy(tag + "own", deps, block, own.indirect(T.slo[:, rank * 16:(rank + 1) * 16]))
         for j, cl in enumerate(calls):
             def fn(e, cl=cl):
                 trs = []
@@ -185,120 +250,114 @@ def steps(g, core, T, topo):
             add("%ssend%d" % (tag, j), sorted(set(made[d] for d, m in cl)), fn, 0)
         add(tag + "in", [], None, 0, (sem, landed))
 
-    swap("x", T.xtab, T.xtab[:, 0:TN], T.slo, T.xs, S.xa, ["ld_hf", "slo"])
+    swap("x", T.xtab, T.xs, S.xa, ["ld_hf", "slo"])
 
-    ee, er = T.b0, T.b1
-    for x in range(2):
-        one("e_a%d" % x, ["ld_p%d" % x], lambda x=x: A.activation(ee[:, 4 * x:384:8], T.ps2[:, 48 * x:48 * x + 48], ACT.Exp))
-        one("e_c%d" % x, ["ld_p%d" % x],
-            lambda x=x: A.activation(ee[:, 4 * x + 1:384:8], T.ps2[:, 48 * x:48 * x + 48], ACT.Exp, scale=0.25))
-    exps = ["e_a0", "e_a1", "e_c0", "e_c1"]
-    one("e_ia", exps, lambda: V.reciprocal(ee[:, 3:384:4], ee[:, 0:384:4]))
-    one("e_ic", exps, lambda: V.reciprocal(ee[:, 2:384:4], ee[:, 1:384:4]))
-    one("p_hi", ["e_ia", "e_ic"], lambda: V.tensor_copy(T.pp[:, 0::4], ee[:, 0:384]))
-    one("p_r", ["p_hi"], lambda: V.tensor_tensor(er[:, 0:384], ee[:, 0:384], T.pp[:, 0::4], OP.subtract))
-    one("p_mid", ["p_r"], lambda: V.tensor_copy(T.pp[:, 1::4], er[:, 0:384]))
-    one("p_lo", ["p_mid"], lambda: V.tensor_tensor(T.pp[:, 2::4], er[:, 0:384], T.pp[:, 1::4], OP.subtract))
-    one("p_t", ["p_lo", "m_pp"], lambda: V.transpose(T.sp[:], T.pp[:]))
-    one("sl_1", ["ld_sl"], lambda: V.tensor_scalar(T.slf[:], T.sl32[:], 1.0 / 48, -23.5 / 48, OP.mult, OP.add))
-    one("sl_2", ["sl_1"], lambda: V.tensor_copy(T.sld[:], T.slf[:]))
-    one("sl_3", ["sl_2"], lambda: V.tensor_scalar(T.slf[:], T.sld[:], -47.96875, None, OP.mult))
-    one("sl_4", ["sl_3"], lambda: V.tensor_tensor(T.slf[:], T.slf[:], T.sl32[:], OP.add))
-    one("sl_5", ["sl_4"], lambda: V.tensor_scalar(T.slp[:], T.slf[:], 32.0, None, OP.mult))
-    swap("s", T.stab, T.sp[:, 0:TN], T.slp, T.ss, S.sa, ["p_t", "sl_5"])
-    one("o_a", [], lambda: g.iota(T.pa[:, 0:96], [[1, 32], [0, 3]], 0, 32))
-    one("o_b", [], lambda: g.iota(T.pa[:, 96:192], [[0, 32], [512, 3]], 0, 0))
-    one("o_c", ["o_a"], lambda: V.tensor_scalar(T.pb[:], T.pa[:, 0:96], 511, None, OP.bitwise_and))
-    one("o_d", ["o_b", "o_c"], lambda: V.tensor_tensor(T.pb[:], T.pb[:], T.pa[:, 96:192], OP.add))
-    one("o_e", ["o_d"], lambda: V.tensor_copy(T.po[:], T.pb[:]))
-    for i in range(2):
-        copy("o_g%d" % i, ["p_t", "o_e"], T.stab[:, i * 768:(i + 1) * 768], T.sp[:, 0:TN].indirect(T.po[:, i * 48:(i + 1) * 48]))
+    one("t_s", ["ld_ps", "c_perm"], lambda: PE.matmul(T.rq[:, 0:96], T.p96[0:96, :], T.turn[0:96, :], True, True))
+    one("e_a", ["t_s"], lambda: A.activation(T.b0[:, 0:384:4], T.rq[:, 0:96], ACT.Exp))
+    one("e_c", ["t_s"], lambda: A.activation(T.b0[:, 1:384:4], T.rq[:, 0:96], ACT.Exp, scale=0.25))
 
-    add("t_d", ["ld_pd", "c_id"],
-        lambda e: [PE.transpose(T.q[:, 0, 416 + t * 8:424 + t * 8], T.pd8[:, t * 128:(t + 1) * 128], T.id32[0:8, 0:8])
-                   for t in range(12)], 12)
-    one("f_e", ["t_d"], lambda: A.activation(T.f2[:, :, 0, :], T.q[:, 0, 416:512], ACT.Exp, scale=-0.75))
-    one("m_q", ["f_e"], lambda: V.memset(T.q[:, :, K:4 * GK:KS], 0.0))
-    one("f_i", ["f_e"], lambda: V.reciprocal(T.f2[:, :, 1, :], T.f2[:, :, 0, :]))
+    def inverse(name, deps, out, x, y, t, u):
+        one(name + "t", deps, lambda: V.tensor_tensor(t, x, y, OP.mult))
+        one(name + "u", [name + "t"], lambda: V.tensor_scalar(u, t, -1.0, 2.0, OP.mult, OP.add))
+        one(name, [name + "u"], lambda: V.tensor_tensor(out, u, y, OP.mult))
+    one("e_ya", ["t_s"], lambda: A.activation(T.y0[:, 0:96], T.rq[:, 0:96], ACT.Exp, scale=-1.0))
+    one("e_yc", ["t_s"], lambda: A.activation(T.y0[:, 96:192], T.rq[:, 0:96], ACT.Exp, scale=-0.25))
+    exps = ["e_a", "e_c", "e_ya", "e_yc"]
+    inverse("ia", exps, T.b0[:, 3:384:4], T.b0[:, 0:384:4], T.y0[:, 0:96], T.b0[:, 512:608], T.b0[:, 512:608])
+    inverse("ic", exps, T.b0[:, 2:384:4], T.b0[:, 1:384:4], T.y0[:, 96:192], T.b0[:, 608:704], T.b0[:, 608:704])
+    for i in range(3):
+        ee, er = T.b0[:, i * 128:(i + 1) * 128], T.b0[:, 512 + i * 128:640 + i * 128]
+        hi, mid, lo = [T.pp[:, i * 512 + j:(i + 1) * 512:4] for j in range(3)]
+        copy("p_hi%d" % i, ["ia", "ic"], hi, ee)
+        one("p_r%d" % i, ["p_hi%d" % i], lambda er=er, ee=ee, hi=hi: V.tensor_tensor(er, ee, hi, OP.subtract))
+        copy("p_mid%d" % i, ["p_r%d" % i], mid, er)
+        one("p_lo%d" % i, ["p_mid%d" % i], lambda er=er, mid=mid, lo=lo: V.tensor_tensor(lo, er, mid, OP.subtract))
+        add("p_t%d" % i, ["p_lo%d" % i, "m_pp", "c_id"],
+            lambda e, i=i: [PE.matmul(T.q[:, i, j * 128:(j + 1) * 128], T.pp[:, (4 * i + j) * 128:(4 * i + j + 1) * 128],
+                                      T.ident[:], True, True) for j in range(4)], 4)
+        copy("p_c%d" % i, ["p_t%d" % i], T.stab[:, i * 512:(i + 1) * 512], T.q[:, i, :])
+    swap("s", T.stab, T.ss, S.sa, ["p_c0", "p_c1", "p_c2", "slo"])
+
+    fq = T.b1[:, 0:96]
+    one("t_d", ["ld_pd", "c_perm"], lambda: PE.matmul(fq, T.d96[0:96, :], T.turn[0:96, :], True, True))
+    one("f_e", ["t_d"], lambda: A.activation(T.f2[:, :, 0, :], fq, ACT.Exp, scale=-0.75))
+    one("f_y", ["t_d"], lambda: A.activation(T.b1[:, 512:608], fq, ACT.Exp, scale=0.75))
+    inverse("f_i", ["f_e", "f_y"], T.f2[:, :, 1, :], T.f2[:, :, 0, :], T.b1[:, 512:608], T.y0[:, 192:288], T.y0[:, 288:384])
+    one("m_q", ["p_c0", "p_c1", "p_c2"], lambda: V.memset(T.q[:, :, K:4 * GK:KS], 0.0))
     for k in range(K):
         copy("f_r%d" % k, ["f_i"], T.frep[:, k::KS], T.f2[:], 192)
     frep = ["f_r%d" % k for k in range(K)] + ["m_fr"]
-    one("offx", ["ld_ed"], lambda: V.tensor_copy(T.offx[:], T.ed32[:]))
-    for p in range(6):
-        one("offs%d" % p, ["ld_ed"],
-            lambda p=p: V.tensor_copy(T.offs[:, p * 192:(p + 1) * 192], T.ed32[:, :, p * 16:(p + 1) * 16]))
-    one("i_b", [], lambda: g.iota(T.ci[:, 160:672], [[-32, 4], [-1, 8], [0, 16]], 0, 1))
-    one("b_and", ["i_b"], lambda: V.tensor_scalar(T.cj[:, 160:672], T.ci[:, 160:672], 0xFFE7, None, OP.bitwise_and))
-    one("b_eq", ["b_and"], lambda: V.tensor_scalar(T.cb[:, 160:672], T.cj[:, 160:672], 0.0, None, OP.is_equal))
+    for c in range(NC):
+        one("off%d" % c, ["ld_ed"],
+            lambda c=c: V.tensor_copy(T.off[:, c * K * CL:(c + 1) * K * CL], T.ed32[:, :, c * CL:(c + 1) * CL]))
+    one("i_b", [], lambda: g.iota(T.ci[:, 32:544], [[-32, 4], [-1, 8], [0, 16]], 0, 1))
+    one("b_and", ["i_b"], lambda: V.tensor_scalar(T.cj[:, 32:544], T.ci[:, 32:544], 0xFFE7, None, OP.bitwise_and))
+    one("b_eq", ["b_and"], lambda: V.tensor_scalar(T.cb[:, 32:544], T.cj[:, 32:544], 0.0, None, OP.is_equal))
 
-    for a, b in XR:
-        for k in range(K):
-            copy("x%d_%d" % (a, k), ["xin", "xown", "m_xz", "offx"], T.xg[:, a * KS + k:b * KS:KS],
-                 T.xtab[:, 0:Z + 8].indirect(T.offx[:, k * 96 + a // 16:k * 96 + b // 16]))
-    for p in range(6):
+    for c in range(NC):
+        for a, b in XR[c]:
+            for k in range(K):
+                o = (c * K + k) * CL
+                copy("x%d_%d_%d" % (c, a, k), ["xin", "xown", "m_xz", "off%d" % c],
+                     T.xg[:, (c * CN + a) * KS + k:(c * CN + b) * KS:KS],
+                     T.xtab[:, 0:Z + 8].indirect(T.off[:, o + a // 16:o + b // 16]))
         for a, b in SK:
-            copy("s%d_%d" % (p, a), ["sin", "sown", "o_g0", "o_g1", "z_col", "offs%d" % p],
-                 T.sg[:, (p * K + a) * 256:(p * K + b) * 256],
-                 T.stab[:, 0:Z + 8].indirect(T.offs[:, (p * K + a) * 16:(p * K + b) * 16]))
+            copy("s%d_%d" % (c, a), ["sin", "sown", "z_col", "off%d" % c], T.sg[:, (c * K + a) * CN:(c * K + b) * CN],
+                 T.stab[:, 0:Z + 8].indirect(T.off[:, (c * K + a) * CL:(c * K + b) * CL]))
 
-    last = ["m_q"] * 4
+    qa, qw, qi = T.q[:, :, 0:GK], T.q[:, :, GK:2 * GK], T.q[:, :, 3 * GK:4 * GK]
+    qr = T.rq[:, 0:NT * GK]
+    for c in range(NC):
+        s, t0 = str(c), c * NT
+        before = str(c - 1)
+        hi, mid, lo = [T.rb[:, t0:t0 + NT, j, :] for j in range(3)]
+        for a, b in SK:
+            add("cm%d_%d" % (c, a), ["s%d_%d" % (c, a), "c_eq", "r" + before if c else "m_q"],
+                lambda e, a=a, b=b, c=c: [
+                    PE.matmul(T.q[:, j, k:4 * GK:KS], T.sg[:, (c * K + k) * CN + j * 128:(c * K + k) * CN + (j + 1) * 128],
+                              sel, True, True) for k in range(a, b) for j in range(NT)], NT * (b - a))
+        one("tt" + s, ["cm%d_%d" % (c, a) for a, b in SK] + frep,
+            lambda t0=t0: V.tensor_tensor(T.tt[:], T.q[:, :, GK:3 * GK], T.frep[:, t0 * 2 * GK:(t0 + NT) * 2 * GK], OP.mult))
+        one("w" + s, ["tt" + s], lambda: V.tensor_tensor(qw, qa, T.tt[:, :, 0:GK], OP.max))
+        one("wi" + s, ["tt" + s], lambda: V.tensor_tensor(T.wi[:], qi, T.tt[:, :, GK:2 * GK], OP.min))
+        r = T.r32[:, t0 * GK:(t0 + NT) * GK]
+        one("r" + s, ["w" + s, "wi" + s], lambda r=r: V.tensor_tensor(r, T.q[:, :, GK - 1:2 * GK - 1], T.wi[:], OP.mult))
+        one("dn" + s, ["r" + s, "rc" + before if c else "m_ones"], lambda r=r: V.tensor_tensor_scan(T.dn[:], r, T.ones[:], 0.0, OP.mult, OP.add))
+        one("rc" + s, ["dn" + s], lambda t0=t0: V.reciprocal(T.r32[:, t0 * GK + K:(t0 + NT) * GK:KS], T.dn[:, K - 1::KS]))
+        copy("hi" + s, ["rc" + s], hi, r, NT * GK)
+        add("rm" + s, ["hi" + s, "c_neg", "c_id32"] + (["lo" + before] if c else exps),
+            lambda e, r=r, hi=hi, c=c: [PE.matmul(qr, T.id32[:], r, True, False), PE.matmul(qr, T.neg[:], hi, False, LO[c] == "v")], 2)
+        copy("md" + s, ["rm" + s], mid, qr)
+        if LO[c] == "v":
+            one("lo" + s, ["md" + s], lambda mid=mid, lo=lo: V.tensor_tensor(lo, qr, mid, OP.subtract))
+        else:
+            one("rl" + s, ["md" + s], lambda mid=mid: PE.matmul(qr, T.neg[:], mid, False, True))
+            copy("lo" + s, ["rl" + s], lo, qr)
 
-    def ratios(s, t0, nt, o):
-        qa, qw, qr, qi = [T.q[:, o:o + nt, i * GK:(i + 1) * GK] for i in range(4)]
-        wi = T.wi[:, o * GK:(o + nt) * GK]
-        hi, mid, lo = [T.rb[:, t0:t0 + nt, j, :] for j in range(3)]
-        cms = []
-        for p in range(t0 // 2, (t0 + nt) // 2):
-            bank = o + 2 * p - t0
-            for a, b in SK:
-                cms.append("cm%d_%d" % (p, a))
-                add(cms[-1], ["s%d_%d" % (p, a), "c_eq", last[bank]],
-                    lambda e, a=a, b=b, p=p, bank=bank: [
-                        PE.matmul(T.q[:, bank + j, k:4 * GK:KS],
-                                  T.sg[:, (p * K + k) * 256 + j * 128:(p * K + k) * 256 + (j + 1) * 128], sel, True, True)
-                        for k in range(a, b) for j in range(2)], 2 * (b - a))
-            last[bank] = "lo" + s
-        one("tt" + s, cms + frep, lambda: V.tensor_tensor(T.tt[:, o:o + nt, :], T.q[:, o:o + nt, GK:3 * GK],
-                                                          T.frep[:, t0 * 2 * GK:(t0 + nt) * 2 * GK], OP.mult))
-        one("w" + s, ["tt" + s], lambda: V.tensor_tensor(qw, qa, T.tt[:, o:o + nt, 0:GK], OP.max))
-        one("wi" + s, ["tt" + s], lambda: V.tensor_tensor(wi, qi, T.tt[:, o:o + nt, GK:2 * GK], OP.min))
-        one("r" + s, ["w" + s, "wi" + s], lambda: V.tensor_tensor(qr, T.q[:, o:o + nt, GK - 1:2 * GK - 1], wi, OP.mult))
-        add("dn" + s, ["r" + s, "m_ones"],
-            lambda e: [V.tensor_tensor_scan(T.dn[:, j * GK:(j + 1) * GK], T.q[:, j, 2 * GK:3 * GK], T.ones[:],
-                                            0.0, OP.mult, OP.add) for j in range(o, o + nt)], nt)
-        one("rc" + s, ["dn" + s],
-            lambda: V.reciprocal(T.q[:, o:o + nt, 2 * GK + K:3 * GK:KS], T.dn[:, o * GK + K - 1:(o + nt) * GK:KS]))
-        copy("hi" + s, ["rc" + s], hi, qr)
-        one("rm" + s, ["hi" + s], lambda: V.tensor_tensor(qw, qr, hi, OP.subtract))
-        copy("md" + s, ["rm" + s], mid, qw)
-        one("lo" + s, ["md" + s], lambda: V.tensor_tensor(lo, qw, mid, OP.subtract))
-
-    t0 = 0
-    for c, (nt, o, turn) in enumerate(CHUNKS):
-        ratios("%d" % c, t0, nt, o)
-        t0 += nt
-        if not turn:
-            continue
-        t1 = t0 - turn
-        add("tp%d" % c, ["lo%d" % c, "m_rb"] + (["lo%d" % (c - 1)] if turn > nt else []),
+    holder = [["p_lo2", "p_lo1", "p_lo0", "f_i"]] * 4
+    for i, (c0, c1) in enumerate(TURNS):
+        t1, t0 = c0 * NT, c1 * NT
+        add("tp%d" % i, ["lo%d" % c for c in range(c0, c1)] + ["m_rb"],
             lambda e, t0=t0, t1=t1: [V.transpose(T.rr[:, t1 * QU + k:t0 * QU:KS], T.rb[:, t1:t0, :, k::KS]) for k in range(KS)], KS)
         for t in range(t1, t0):
-            w = 2 * (t % RING) * HU
-            for h in range(2):
-                u = 2 * t + h
-                buf = T.b1 if h else T.b0
-                add("bc%d" % u, ["tp%d" % c, "b_eq"] + (["sc%d" % (u - 2)] if u >= 2 else []),
-                    lambda e, buf=buf, o=t * QU, h=h: [
-                        PE.matmul(buf[:, j * QU + a:j * QU + b], T.cb[:, 160 + (2 * h + j) * 128:288 + (2 * h + j) * 128],
-                                  T.rr[:, o + a:o + b], True, True)
-                        for j, a, b in ((0, 0, QU), (1, 0, 512 - QU), (1, 512 - QU, QU))], 3)
-                a = [a for a, b in XR if a <= u * 64 < b][0]
-                one("sc%d" % u, ["bc%d" % u, "m_xg"] + ["x%d_%d" % (a, k) for k in range(K)]
+            w = 4 * (t % RING) * QU
+            per = 4 // WIDE
+            for h in range(per):
+                u = per * t + h
+                buf, o = (T.b0, T.b1)[h * WIDE // 2], 512 + (h * WIDE % 2 - 1) * QU
+                add("bc%d" % u, ["tp%d" % i, "b_eq"] + holder[h],
+                    lambda e, buf=buf, o=o, t=t, h=h * WIDE: [
+                        PE.matmul(buf[:, o + j * QU:o + (j + 1) * QU], T.cb[:, 32 + (h + j) * 128:160 + (h + j) * 128],
+                                  T.rr[:, t * QU:(t + 1) * QU], True, True) for j in range(WIDE)], WIDE)
+                holder[h] = ["sc%d" % u]
+                c = t // NT
+                a = [a for a, b in XR[c] if a <= u * 32 * WIDE - c * CN < b][0]
+                one("sc%d" % u, ["bc%d" % u, "m_xg"] + ["x%d_%d_%d" % (c, a, k) for k in range(K)]
                     + (["ex%d" % (t - RING)] if t >= RING else []),
-                    lambda u=u, buf=buf, w=w + h * HU: V.tensor_tensor_scan(T.st[:, w:w + HU], buf[:, 0:HU],
-                                                                            T.xg[:, u * HU:(u + 1) * HU], 0.0, OP.mult, OP.add))
-            copy("ex%d" % t, ["sc%d" % (2 * t), "sc%d" % (2 * t + 1)], T.yb[:, t * 128:(t + 1) * 128],
-                 T.st[:, w + K:w + 2 * HU:KS], 128)
+                    lambda u=u, buf=buf, o=o, w=w + h * WIDE * QU, n=WIDE * QU: V.tensor_tensor_scan(
+                        T.st[:, w:w + n], buf[:, o:o + n], T.xg[:, u * n:(u + 1) * n], 0.0, OP.mult, OP.add))
+            copy("ex%d" % t, ["sc%d" % (per * t + h) for h in range(per)], T.yb[:, t * 128:(t + 1) * 128],
+                 T.st[:, w + K:w + 4 * QU:KS], 128)
             if t % 2 or t >= 10:
                 a, b = (t if t >= 10 else t - 1) * 128, (t + 1) * 128
                 dma("out%d" % t, ["ex%d" % i for i in range(a // 128, t + 1)], T.y[:, a:b], T.yb[:, a:b], S.stored, False)
@@ -311,7 +370,7 @@ def rank_program(g, core, T, topo):
         return
     S = T.sem
     tasks, sent = steps(g, core, T, topo)
-    queues = {e: ORDER[e].split() for e in ORDER}
+    queues = order(tasks)
     cnt = {"v": S.cv, "s": S.cs, "t": S.ct, "g": S.cg}
     token = {}
     total = {}

from concourse.bass import DstId, RemoteDMATransfer
from concourse.mybir import AluOpType, AxisListType, ActivationFunctionType

N, TN, M, K = 8, 1536, 256, 12
Z = TN + N * M
KS = K + 1
QU = 32 * KS
HU = 64 * KS
GK = 8 * KS
RING = 4
NT = 3
NC = 12 // NT
CN = 128 * NT
CL = CN // 16
TURNS = [(0, 1), (1, 3), (3, 4)]
XR = [[(0, CN)], [(0, CN)], [(0, CN)], [(0, 256), (256, CN)]]
SK = [(0, 3), (3, 6), (6, 9), (9, 12)]
GATHERS = "s0 s1 x0 s2 s3 x1 x2 x3"
GATHER, CALL, TENSOR, WAKE, PATIENCE, PARTS = 1.6, 70, 1.0, 170, 200, 5000
LO, MD = "vvvv", "ssss"
SHORT = 15
SOON = 300
FIRST = 8
WIDE = 1
SHARE = 0.23
START = {
    "v": "m_ones m_xz m_pp m_fr m_rb b_and c_and b_eq slo c_eq c_neg z_a z_ai z_ci xg1 iat ict z_sum iau icu z_col ia ic "
         "p_hi0 p_hi1 p_r0 p_hi2 p_mid0 p_r1 p_lo0 p_mid1 p_r2 p_lo1 p_mid2 f_it p_lo2 f_iu f_i off0 p_c2 sg1 sg3 m_q off1 off2 off3",
    "s": "ld_sl z_big c_id32 e_c e_yc e_a e_ya xg0 xg2 xg3 f_e f_y xown p_c0 p_c1 sg0 sg2 sown",
    "t": "t_s t_d p_t0 p_t1 p_t2",
    "g": "i_b c_perm i_s c_id xsend0 xsend1 ssend0 ssend1 f_r0 f_r1 f_r2 f_r3 f_r4 f_r5 f_r6 f_r7 f_r8 f_r9 f_r10 f_r11 m_xg",
    "y": "ld_ps ld_hf ld_pd ld_ed out1 out3 out5 out7 out9 out10 out11",
}

SCRATCH = {
    "xtab": ("sbuf", [128, 3600], "bfloat16"),
    "stab": ("sbuf", [128, 3600], "bfloat16"),
    "xs": ("sbuf", [128, N * M], "bfloat16"),
    "ss": ("sbuf", [128, N * M], "bfloat16"),
    "sl32": ("sbuf", [128, 128], "int32"),
    "slo": ("sbuf", [128, 128], "uint16"),
    "ed32": ("sbuf", [128, K, 96], "int32"),
    "off": ("sbuf", [128, K * 96], "uint16"),
    "p96": ("sbuf", [128, 128], "float32"),
    "d96": ("sbuf", [128, 128], "float32"),
    "turn": ("sbuf", [128, 96], "float32"),
    "ident": ("sbuf", [128, 128], "bfloat16"),
    "neg": ("sbuf", [128, 128], "bfloat16"),
    "id32": ("sbuf", [128, 128], "float32"),
    "y0": ("sbuf", [128, 384], "float32"),
    "r32": ("sbuf", [128, 12 * GK], "float32"),
    "ci": ("sbuf", [128, 544], "int32"),
    "cj": ("sbuf", [128, 544], "int32"),
    "cb": ("sbuf", [128, 544], "bfloat16"),
    "ones": ("sbuf", [128, NT * GK], "float32"),
    "big": ("sbuf", [128, 4], "float32"),
    "zt": ("sbuf", [128, 24], "float32"),
    "zc": ("sbuf", [128, 4], "float32"),
    "pp": ("sbuf", [128, TN], "bfloat16"),
    "f2": ("sbuf", [128, 12, 2, 8], "float32"),
    "frep": ("sbuf", [128, 24 * GK], "float32"),
    "xg": ("sbuf", [128, TN * KS], "bfloat16"),
    "sg": ("sbuf", [128, TN * K], "bfloat16"),
    "st": ("sbuf", [128, RING * 2 * HU], "float32"),
    "tt": ("sbuf", [128, NT, 2 * GK], "float32"),
    "wi": ("sbuf", [128, NT * GK], "float32"),
    "dn": ("sbuf", [128, NT * GK], "float32"),
    "rb": ("sbuf", [128, 12, 4, GK], "bfloat16"),
    "rr": ("sbuf", [128, 12 * QU], "bfloat16"),
    "yb": ("sbuf", [128, TN], "float32"),
    "q": ("psum", [128, NT, 512], "float32"),
    "rq": ("psum", [128, 512], "float32"),
    "b0": ("psum", [128, 1024], "float32"),
    "b1": ("psum", [128, 1024], "float32"),
}
SEMAPHORES = ["cv", "cs", "ct", "cg", "l_sl", "l_hf", "l_ed", "l_ps", "l_pd", "xa", "sa", "sent", "stored"]


def order(tasks):
    xs = [["x%d_%d_%d" % (c, a, k) for a, b in XR[c] for k in range(K)] for c in range(NC)]
    ss = [["s%d_%d" % (c, a) for a, b in SK] for c in range(NC)]
    lists = {"x": xs, "s": ss}
    gathers = [n for part in GATHERS.split() for n in lists[part[0]][int(part[1])]]
    cost = {}
    for c in range(NC):
        for a, b in XR[c]:
            cost.update({"x%d_%d_%d" % (c, a, k): CALL + GATHER * (b - a) for k in range(K)})
        for a, b in SK:
            cost["s%d_%d" % (c, a)] = CALL + GATHER * CN * (b - a)
            cost["cm%d_%d" % (c, a)] = TENSOR * 64 * NT * (b - a)
        for n, w in (("tt", 2), ("w", 1), ("wi", 1), ("r", 1), ("dn", 1), ("rc", 1.2), ("md", 1.25), ("lo", 1), ("hi", 2.7),
                     ("rm", 5 * TENSOR)):
            cost[n + str(c)] = w * NT * GK + SHORT
    for i, (a, b) in enumerate(TURNS):
        cost["tp%d" % i] = KS * (max(64, 16 * NT * (b - a)) + SHORT)
    scans = 48 // WIDE
    for u in range(scans):
        cost["sc%d" % u], cost["bc%d" % u], cost["ex%d" % (u % 12)] = WIDE * QU + SHORT, TENSOR * WIDE * QU, 510

    def each(names, n):
        return [a + str(i) for i in range(n) for a in names.split()]
    own = each("lo", NC) + each("tp", len(TURNS)) + each("tt w wi r dn rc", NC) + each("sc", scans) + ["ex11"]
    first = xs[0][:FIRST]
    prefer = {"v": own + first + gathers, "s": each("md", NC) + [n for n in gathers if n not in first],
              "t": each("rm", NC) + ["cm" + n[1:] for c in ss for n in c] + each("bc", scans), "g": each("hi", NC) + each("ex", 11)}
    for c in range(NC):
        if LO[c] == "s":
            prefer["v"].remove("lo%d" % c)
            prefer["s"].insert(0, "lo%d" % c)
            prefer["t"].insert(0, "rl%d" % c)
            cost["rl%d" % c] = TENSOR * NT * GK
        if MD[c] == "v":
            prefer["s"].remove("md%d" % c)
            prefer["v"].insert(0, "md%d" % c)
    queues = {e: START[e].split() for e in START}
    done = {n: 0 for e in queues for n in queues[e]}
    done["xin"], done["sin"] = 0, PARTS
    free = {e: 0 for e in prefer}
    left = set(cost)
    share = SHARE * sum(cost[n] for n in gathers)
    while left:
        e = min(free, key=lambda k: free[k])
        ready = {n: max(done[d] for d in tasks[n][0]) + WAKE for n in prefer[e]
                 if n in left and all(d in done for d in tasks[n][0])}
        now = [n for n in prefer[e] if n in ready and ready[n] <= free[e] + (PATIENCE if n not in gathers else 0)]
        if e == "v" and share <= 0:
            now = [n for n in now if n not in gathers]
        if e == "v" and any(ready[n] <= free[e] + SOON for n in ready if n not in gathers):
            now = [n for n in now if n not in lists["s"][0] + lists["s"][1] + lists["s"][2] + lists["s"][3]]
        now = [n for n in now if ready[n] <= free[e] and n not in gathers] + now
        if not now:
            free[e] += 20
            continue
        n = now[0]
        if e == "v" and n in gathers:
            share -= cost[n]
        free[e] = done[n] = max(free[e], ready[n]) + cost[n]
        queues[e].append(n)
        left.remove(n)
    return queues


def exchange(src, cores, topo):
    others = [d for d in range(len(cores)) if cores[d] != src]
    far = [d for d in others if topo.host(cores[d]) != topo.host(src)]
    home = [d for d in others if cores[d] in topo.cores_of(src)]
    near = [d for d in others if d not in far and d not in home]
    calls = []
    used = set()
    for grp in (far, near):
        eng = topo.engines(src, cores[grp[0]])
        n = len(eng) // len(grp)
        calls.append([(d, sum(1 << e for e in eng[i * n:(i + 1) * n])) for i, d in enumerate(grp)])
        used.update(eng)
    free = [e for e in topo.engines(src, cores[home[0]]) if e not in used]
    calls[1].append((home[0], sum(1 << e for e in free[::2])))
    return calls, far, near, home


def steps(g, core, T, topo):
    rank = T.rank_of(core)
    cores = list(T.cores)
    S = T.sem
    ACT, OP = ActivationFunctionType, AluOpType
    V, A, PE = g.vector, g.scalar, g.tensor
    tasks = {}

    def add(name, deps, fn, n=1, tok=None):
        tasks[name] = (list(deps), fn, n, tok)

    def one(name, deps, fn):
        add(name, deps, lambda e: [fn()])

    def copy(name, deps, out, src, n=0):
        def fn(e):
            if e == "v":
                return [V.tensor_copy(out, src)]
            if e == "s":
                return [A.activation(out, src, ACT.Copy)]
            return [g.affine_select(out, src, [[0, n]], OP.is_ge, 0.0, 0, 0)]
        add(name, deps, fn)

    def zero(name, out, n=0):
        add(name, [], lambda e: [V.memset(out, 0.0) if e == "v" else
                                 g.iota(out, [[0, n]], 0, 0, allow_small_or_imprecise_dtypes=True)])

    def dma(name, deps, out, src, sem, tok=True):
        def fn(e):
            (g.sync if e == "y" else A).dma_start(out, src).then_inc(sem, 16)
            return []
        add(name, deps, fn, 0, (sem, 16) if tok else None)

    dma("ld_ps", [], T.p96[0:96, :], T.ps[:], S.l_ps)
    dma("ld_pd", [], T.d96[0:96, :], T.pd[:], S.l_pd)
    dma("ld_sl", [], T.sl32[:], T.sl[:], S.l_sl)
    dma("ld_hf", [], T.xtab[:, 0:TN], T.hf[:], S.l_hf)
    dma("ld_ed", ["ld_hf"], T.ed32[:], T.ed[:], S.l_ed)

    sel = T.cb[:, 0:32]
    one("m_ones", [], lambda: V.memset(T.ones[:], 1.0))
    one("c_perm", ["m_ones"], lambda: g.affine_select(T.turn[:], T.ones[:, 0:96], [[-1, 12], [-12, 8]], OP.is_equal, 0.0, 0, 1))
    one("c_id", ["m_ones"], lambda: g.affine_select(T.ident[:], T.ones[:, 0:128], [[-1, 128]], OP.is_equal, 0.0, 0, 1))
    one("c_neg", ["c_id"], lambda: V.tensor_scalar(T.neg[:], T.ident[:], -1.0, None, OP.mult))
    copy("c_id32", ["c_id"], T.id32[:], T.ident[:])
    one("i_s", [], lambda: g.iota(T.ci[:, 0:32], [[-32, 4], [-128, 8]], 0, 8))
    one("c_and", ["i_s"], lambda: V.tensor_scalar(T.cj[:, 0:32], T.ci[:, 0:32], 0xFFE7, None, OP.bitwise_and))
    one("c_eq", ["c_and"], lambda: V.tensor_scalar(sel, T.cj[:, 0:32], 0.0, None, OP.is_equal))
    zero("m_xz", T.xtab[:, Z:Z + 8])
    zero("m_pp", T.pp[:, 3::4])
    zero("m_xg", T.xg[:, K::KS], TN)
    zero("m_rb", T.rb[:, :, 3, :], 12 * GK)
    zero("m_fr", T.frep[:, K::KS])
    one("z_big", ["m_ones"], lambda: A.activation(T.big[:], T.ones[:, 0:4], ACT.Exp, scale=35.0))
    one("z_a", ["c_eq"], lambda: V.tensor_scalar(T.zt[:, 0:8], T.cb[:, 0:8], 2.0 ** -42, None, OP.mult))
    one("z_ai", ["c_eq"], lambda: V.tensor_scalar(T.zt[:, 8:16], T.cb[:, 24:32], 2.0 ** 38, None, OP.mult))
    one("z_ci", ["c_eq", "z_big"], lambda: V.tensor_scalar(T.zt[:, 16:24], T.cb[:, 16:24], T.big[:, 0:1], None, OP.mult))
    one("z_sum", ["z_a", "z_ai", "z_ci"], lambda: V.tensor_reduce(T.zc[:, 0:1], T.zt[:], AxisListType.X, OP.add))
    one("z_col", ["z_sum", "m_ones"], lambda: V.tensor_scalar(T.stab[:, Z:Z + 8], T.ones[:, 0:8], T.zc[:, 0:1], None, OP.mult))

    calls, far, near, home = exchange(core, cores, topo)
    landed = 0
    for c in cores:
        if c != core:
            for cl in exchange(c, cores, topo)[0]:
                landed += sum(bin(m).count("1") for d, m in cl if d == rank)
    one("slo", ["ld_sl"], lambda: V.tensor_copy(T.slo[:], T.sl32[:]))

    def swap(tag, tab, stage, sem, deps):
        own = tab[:, 0:TN]
        made = {}
        for grp in (far, near, home):
            for i in range(0, len(grp), 2):
                d, n = grp[i], len(grp[i:i + 2])
                assert grp[i + n - 1] == d + n - 1
                name = "%sg%d" % (tag, len(set(made.values())))
                copy(name, deps, stage[:, d * M:(d + n) * M], own.indirect(T.slo[:, d * 16:(d + n) * 16]))
                for j in range(n):
                    made[d + j] = name
        block = tab[:, TN + rank * M:TN + (rank + 1) * M]
        copy(tag + "own", deps, block, own.indirect(T.slo[:, rank * 16:(rank + 1) * 16]))
        for j, cl in enumerate(calls):
            def fn(e, cl=cl):
                trs = []
                for d, m in cl:
                    rid, pid = topo.addr(cores[d], core)
                    trs.append(RemoteDMATransfer(dst_ids=[DstId(rid=rid, pnc=pid)], dma_engine_mask=m, remote_sem=sem,
                                                 src=stage[:, d * M:(d + 1) * M], dst=block))
                g.remote_dma_fused(trs, local_sem=S.sent)
                return []
            add("%ssend%d" % (tag, j), sorted(set(made[d] for d, m in cl)), fn, 0)
        add(tag + "in", [], None, 0, (sem, landed))

    swap("x", T.xtab, T.xs, S.xa, ["ld_hf", "slo"])

    one("t_s", ["ld_ps", "c_perm"], lambda: PE.matmul(T.rq[:, 0:96], T.p96[0:96, :], T.turn[0:96, :], True, True))
    one("e_a", ["t_s"], lambda: A.activation(T.b0[:, 0:384:4], T.rq[:, 0:96], ACT.Exp))
    one("e_c", ["t_s"], lambda: A.activation(T.b0[:, 1:384:4], T.rq[:, 0:96], ACT.Exp, scale=0.25))

    def inverse(name, deps, out, x, y, t, u):
        one(name + "t", deps, lambda: V.tensor_tensor(t, x, y, OP.mult))
        one(name + "u", [name + "t"], lambda: V.tensor_scalar(u, t, -1.0, 2.0, OP.mult, OP.add))
        one(name, [name + "u"], lambda: V.tensor_tensor(out, u, y, OP.mult))
    one("e_ya", ["t_s"], lambda: A.activation(T.y0[:, 0:96], T.rq[:, 0:96], ACT.Exp, scale=-1.0))
    one("e_yc", ["t_s"], lambda: A.activation(T.y0[:, 96:192], T.rq[:, 0:96], ACT.Exp, scale=-0.25))
    exps = ["e_a", "e_c", "e_ya", "e_yc"]
    inverse("ia", exps, T.b0[:, 3:384:4], T.b0[:, 0:384:4], T.y0[:, 0:96], T.b0[:, 512:608], T.b0[:, 512:608])
    inverse("ic", exps, T.b0[:, 2:384:4], T.b0[:, 1:384:4], T.y0[:, 96:192], T.b0[:, 608:704], T.b0[:, 608:704])
    for i in range(3):
        ee, er = T.b0[:, i * 128:(i + 1) * 128], T.b0[:, 512 + i * 128:640 + i * 128]
        hi, mid, lo = [T.pp[:, i * 512 + j:(i + 1) * 512:4] for j in range(3)]
        copy("p_hi%d" % i, ["ia", "ic"], hi, ee)
        one("p_r%d" % i, ["p_hi%d" % i], lambda er=er, ee=ee, hi=hi: V.tensor_tensor(er, ee, hi, OP.subtract))
        copy("p_mid%d" % i, ["p_r%d" % i], mid, er)
        one("p_lo%d" % i, ["p_mid%d" % i], lambda er=er, mid=mid, lo=lo: V.tensor_tensor(lo, er, mid, OP.subtract))
        add("p_t%d" % i, ["p_lo%d" % i, "m_pp", "c_id"],
            lambda e, i=i: [PE.matmul(T.q[:, i, j * 128:(j + 1) * 128], T.pp[:, (4 * i + j) * 128:(4 * i + j + 1) * 128],
                                      T.ident[:], True, True) for j in range(4)], 4)
        copy("p_c%d" % i, ["p_t%d" % i], T.stab[:, i * 512:(i + 1) * 512], T.q[:, i, :])
    swap("s", T.stab, T.ss, S.sa, ["p_c0", "p_c1", "p_c2", "slo"])

    fq = T.b1[:, 0:96]
    one("t_d", ["ld_pd", "c_perm"], lambda: PE.matmul(fq, T.d96[0:96, :], T.turn[0:96, :], True, True))
    one("f_e", ["t_d"], lambda: A.activation(T.f2[:, :, 0, :], fq, ACT.Exp, scale=-0.75))
    one("f_y", ["t_d"], lambda: A.activation(T.b1[:, 512:608], fq, ACT.Exp, scale=0.75))
    inverse("f_i", ["f_e", "f_y"], T.f2[:, :, 1, :], T.f2[:, :, 0, :], T.b1[:, 512:608], T.y0[:, 192:288], T.y0[:, 288:384])
    one("m_q", ["p_c0", "p_c1", "p_c2"], lambda: V.memset(T.q[:, :, K:4 * GK:KS], 0.0))
    for k in range(K):
        copy("f_r%d" % k, ["f_i"], T.frep[:, k::KS], T.f2[:], 192)
    frep = ["f_r%d" % k for k in range(K)] + ["m_fr"]
    for c in range(NC):
        one("off%d" % c, ["ld_ed"],
            lambda c=c: V.tensor_copy(T.off[:, c * K * CL:(c + 1) * K * CL], T.ed32[:, :, c * CL:(c + 1) * CL]))
    one("i_b", [], lambda: g.iota(T.ci[:, 32:544], [[-32, 4], [-1, 8], [0, 16]], 0, 1))
    one("b_and", ["i_b"], lambda: V.tensor_scalar(T.cj[:, 32:544], T.ci[:, 32:544], 0xFFE7, None, OP.bitwise_and))
    one("b_eq", ["b_and"], lambda: V.tensor_scalar(T.cb[:, 32:544], T.cj[:, 32:544], 0.0, None, OP.is_equal))

    for c in range(NC):
        for a, b in XR[c]:
            for k in range(K):
                o = (c * K + k) * CL
                copy("x%d_%d_%d" % (c, a, k), ["xin", "xown", "m_xz", "off%d" % c],
                     T.xg[:, (c * CN + a) * KS + k:(c * CN + b) * KS:KS],
                     T.xtab[:, 0:Z + 8].indirect(T.off[:, o + a // 16:o + b // 16]))
        for a, b in SK:
            copy("s%d_%d" % (c, a), ["sin", "sown", "z_col", "off%d" % c], T.sg[:, (c * K + a) * CN:(c * K + b) * CN],
                 T.stab[:, 0:Z + 8].indirect(T.off[:, (c * K + a) * CL:(c * K + b) * CL]))

    qa, qw, qi = T.q[:, :, 0:GK], T.q[:, :, GK:2 * GK], T.q[:, :, 3 * GK:4 * GK]
    qr = T.rq[:, 0:NT * GK]
    for c in range(NC):
        s, t0 = str(c), c * NT
        before = str(c - 1)
        hi, mid, lo = [T.rb[:, t0:t0 + NT, j, :] for j in range(3)]
        for a, b in SK:
            add("cm%d_%d" % (c, a), ["s%d_%d" % (c, a), "c_eq", "r" + before if c else "m_q"],
                lambda e, a=a, b=b, c=c: [
                    PE.matmul(T.q[:, j, k:4 * GK:KS], T.sg[:, (c * K + k) * CN + j * 128:(c * K + k) * CN + (j + 1) * 128],
                              sel, True, True) for k in range(a, b) for j in range(NT)], NT * (b - a))
        one("tt" + s, ["cm%d_%d" % (c, a) for a, b in SK] + frep,
            lambda t0=t0: V.tensor_tensor(T.tt[:], T.q[:, :, GK:3 * GK], T.frep[:, t0 * 2 * GK:(t0 + NT) * 2 * GK], OP.mult))
        one("w" + s, ["tt" + s], lambda: V.tensor_tensor(qw, qa, T.tt[:, :, 0:GK], OP.max))
        one("wi" + s, ["tt" + s], lambda: V.tensor_tensor(T.wi[:], qi, T.tt[:, :, GK:2 * GK], OP.min))
        r = T.r32[:, t0 * GK:(t0 + NT) * GK]
        one("r" + s, ["w" + s, "wi" + s], lambda r=r: V.tensor_tensor(r, T.q[:, :, GK - 1:2 * GK - 1], T.wi[:], OP.mult))
        one("dn" + s, ["r" + s, "rc" + before if c else "m_ones"], lambda r=r: V.tensor_tensor_scan(T.dn[:], r, T.ones[:], 0.0, OP.mult, OP.add))
        one("rc" + s, ["dn" + s], lambda t0=t0: V.reciprocal(T.r32[:, t0 * GK + K:(t0 + NT) * GK:KS], T.dn[:, K - 1::KS]))
        copy("hi" + s, ["rc" + s], hi, r, NT * GK)
        add("rm" + s, ["hi" + s, "c_neg", "c_id32"] + (["lo" + before] if c else exps),
            lambda e, r=r, hi=hi, c=c: [PE.matmul(qr, T.id32[:], r, True, False), PE.matmul(qr, T.neg[:], hi, False, LO[c] == "v")], 2)
        copy("md" + s, ["rm" + s], mid, qr)
        if LO[c] == "v":
            one("lo" + s, ["md" + s], lambda mid=mid, lo=lo: V.tensor_tensor(lo, qr, mid, OP.subtract))
        else:
            one("rl" + s, ["md" + s], lambda mid=mid: PE.matmul(qr, T.neg[:], mid, False, True))
            copy("lo" + s, ["rl" + s], lo, qr)

    holder = [["p_lo2", "p_lo1", "p_lo0", "f_i"]] * 4
    for i, (c0, c1) in enumerate(TURNS):
        t1, t0 = c0 * NT, c1 * NT
        add("tp%d" % i, ["lo%d" % c for c in range(c0, c1)] + ["m_rb"],
            lambda e, t0=t0, t1=t1: [V.transpose(T.rr[:, t1 * QU + k:t0 * QU:KS], T.rb[:, t1:t0, :, k::KS]) for k in range(KS)], KS)
        for t in range(t1, t0):
            w = 4 * (t % RING) * QU
            per = 4 // WIDE
            for h in range(per):
                u = per * t + h
                buf, o = (T.b0, T.b1)[h * WIDE // 2], 512 + (h * WIDE % 2 - 1) * QU
                add("bc%d" % u, ["tp%d" % i, "b_eq"] + holder[h],
                    lambda e, buf=buf, o=o, t=t, h=h * WIDE: [
                        PE.matmul(buf[:, o + j * QU:o + (j + 1) * QU], T.cb[:, 32 + (h + j) * 128:160 + (h + j) * 128],
                                  T.rr[:, t * QU:(t + 1) * QU], True, True) for j in range(WIDE)], WIDE)
                holder[h] = ["sc%d" % u]
                c = t // NT
                a = [a for a, b in XR[c] if a <= u * 32 * WIDE - c * CN < b][0]
                one("sc%d" % u, ["bc%d" % u, "m_xg"] + ["x%d_%d_%d" % (c, a, k) for k in range(K)]
                    + (["ex%d" % (t - RING)] if t >= RING else []),
                    lambda u=u, buf=buf, o=o, w=w + h * WIDE * QU, n=WIDE * QU: V.tensor_tensor_scan(
                        T.st[:, w:w + n], buf[:, o:o + n], T.xg[:, u * n:(u + 1) * n], 0.0, OP.mult, OP.add))
            copy("ex%d" % t, ["sc%d" % (per * t + h) for h in range(per)], T.yb[:, t * 128:(t + 1) * 128],
                 T.st[:, w + K:w + 4 * QU:KS], 128)
            if t % 2 or t >= 10:
                a, b = (t if t >= 10 else t - 1) * 128, (t + 1) * 128
                dma("out%d" % t, ["ex%d" % i for i in range(a // 128, t + 1)], T.y[:, a:b], T.yb[:, a:b], S.stored, False)
    sent = 2 * sum(bin(m).count("1") for cl in calls for d, m in cl)
    return tasks, sent


def rank_program(g, core, T, topo):
    if T.rank_of(core) is None:
        return
    S = T.sem
    tasks, sent = steps(g, core, T, topo)
    queues = order(tasks)
    cnt = {"v": S.cv, "s": S.cs, "t": S.ct, "g": S.cg}
    token = {}
    total = {}
    for e in queues:
        n = 0
        for name in queues[e]:
            if tasks[name][2]:
                n += tasks[name][2]
                token[name] = (e, cnt[e], n)
        total[e] = n
    for name in tasks:
        if tasks[name][3] is not None:
            token[name] = (name,) + tasks[name][3]
    engine = {"v": g.vector, "s": g.scalar, "t": g.tensor, "g": g, "y": g.sync}
    for e in queues:
        seen = {}
        for name in queues[e]:
            need = {}
            for d in tasks[name][0]:
                k, sem, n = token[d]
                if n > seen.get(k, 0) and n > need.get(k, (None, 0))[1]:
                    need[k] = (sem, n)
            for k in need:
                engine[e].wait_ge(need[k][0], need[k][1])
                seen[k] = need[k][1]
            for ins in tasks[name][1](e):
                ins.then_inc(cnt[e], 1)
    for e in "vstg":
        g.wait_ge(cnt[e], total[e])
    g.wait_ge(S.sent, sent)
    g.wait_ge(S.stored, 16 * len([n for n in tasks if n.startswith("out")]))
